import numpy as np
import ml_dtypes


def mxq(x, axis, fmt="e4m3"):
    dtype, down = {"e4m3": (ml_dtypes.float8_e4m3fn, 7), "e5m2": (ml_dtypes.float8_e5m2, 14)}[fmt]
    v = np.moveaxis(np.asarray(x, np.float32).astype(ml_dtypes.bfloat16).astype(np.float64), axis, -1)
    blocks = v.reshape(v.shape[:-1] + (-1, 32))
    amax = np.abs(blocks).max(-1, keepdims=True)
    byte = np.maximum(np.where(amax > 0, np.frexp(amax)[1] - 1 + 127, 0) - down, 1)
    scale = np.exp2(byte - 127.0)
    codes = (blocks / scale).astype(np.float32).astype(dtype).astype(np.float64)
    return np.moveaxis((codes * scale).reshape(v.shape), -1, axis)


WIDE = False


def mx_kscale(k):
    if not WIDE:
        return np.ones(k)
    levels = np.array([10, -10, 5, -5, 0])
    if k % 512:
        return np.exp2(np.random.permutation(np.resize(levels, k // 32))).repeat(32)
    a = np.empty((k // 512, 16))
    for p in range(k // 512):
        a[p, :8] = np.random.permutation(np.resize(levels, 8))
        for g in range(8):
            far = levels[np.abs(levels - a[p, g]) >= 10]
            a[p, g + 8] = far[np.random.randint(len(far))]
    return np.exp2(a.ravel()).repeat(32)


BF16 = ml_dtypes.bfloat16


def bf(x):
    return np.asarray(x, np.float32).astype(BF16)


def f64(x):
    return np.asarray(x).astype(np.float64)


E2M1 = np.array([0.0, 0.5, 1.0, 1.5, 2.0, 3.0, 4.0, 6.0, -0.0, -0.5, -1.0, -1.5, -2.0, -3.0, -4.0, -6.0])


def pack_weight(w, fmt):
    k, n = w.shape
    w = f64(bf(w)).reshape(k // 32, 32, n)
    amax = np.abs(w).max(1)
    if fmt == "e4m3":
        byte = np.frexp(amax)[1] - 1 + 127 - 7
    else:
        mant, ex = np.frexp(amax / 6.0)
        byte = np.where(mant > 0.5, ex, ex - 1) + 127
    byte = np.clip(np.where(amax > 0, byte, 1), 1, 254)
    scaled = (w * np.exp2(127.0 - byte)[:, None, :]).reshape(k, n).astype(np.float32)
    by_word = np.ascontiguousarray(scaled.reshape(k // 512, 128, 4, n).transpose(0, 1, 3, 2))
    if fmt == "e4m3":
        words = by_word.astype(ml_dtypes.float8_e4m3fn).view(np.uint8)
    else:
        c = by_word.astype(ml_dtypes.float4_e2m1fn).view(np.uint8) & 0xF
        words = c[..., 0::2] | (c[..., 1::2] << 4)
    return np.ascontiguousarray(words), np.ascontiguousarray(byte.astype(np.uint8).reshape(k // 512, 16, n))


def unpack_weight(words, scales, fmt):
    g, p, n, _ = words.shape
    if fmt == "e4m3":
        vals = np.ascontiguousarray(words).view(ml_dtypes.float8_e4m3fn).astype(np.float64)
    else:
        nib = np.empty((g, p, n, 4), np.uint8)
        nib[..., 0::2] = words & 0xF
        nib[..., 1::2] = words >> 4
        vals = E2M1[nib]
    vals = vals * np.repeat(np.exp2(scales.astype(np.float64) - 127.0), 8, axis=1)[..., None]
    return vals.transpose(0, 1, 3, 2).reshape(g * 512, n)
def pack4(w):
    words, scales = pack_weight(w, "e2m1")
    return words.reshape(words.shape[0], 128, -1), scales


def unpack4(words, scales):
    return unpack_weight(words.reshape(words.shape[0], 128, -1, 2), scales, "e2m1")


E4M3FN = np.array([(-1.0 if i & 128 else 1.0) * ((1.0 + (i & 7) / 8.0) * 2.0 ** (((i >> 3) & 15) - 7) if i & 120 else (i & 7) * 2.0 ** -9) for i in range(256)])


def e4m3fn_bytes(y):
    return np.clip(np.asarray(y, np.float64), -448.0, 448.0).astype(np.float32).astype(ml_dtypes.float8_e4m3fn).view(np.uint8)


def e4m3fn_values(b):
    return E4M3FN[b]


N, Z, D, H, V = 256, 4, 1024, 1024, 2048


def logsumexp(t, axis, keepdims):
    m = t.max(axis=axis, keepdims=True)
    out = m + np.log(np.sum(np.exp(t - m), axis=axis, keepdims=True))
    return out if keepdims else np.squeeze(out, axis=axis)


def draw0():
    s, t = mx_kscale(D), mx_kscale(H)
    x = bf(np.random.standard_normal((N, Z, D)) * s)
    w1_words, w1_scales = pack4(np.random.standard_normal((D, H)) / np.sqrt(D) / s[:, None])
    b1 = bf(0.3 * np.random.standard_normal(H))
    g = bf((1.0 + 0.1 * np.random.standard_normal(H)) * t)
    e_words, e_scales = pack4(2.0 * np.random.standard_normal((H, V)) / np.sqrt(H) / t[:, None])
    score = bf(np.random.standard_normal((N, Z)))
    return {
        "x": x,
        "w1_words": w1_words,
        "w1_scales": w1_scales,
        "b1": b1,
        "g": g,
        "e_words": e_words,
        "e_scales": e_scales,
        "score": score,
    }


def core(x, w1_words, w1_scales, b1, g, e_words, e_scales, score):
    vocab = e_scales.shape[2]
    a = np.tanh((mxq(f64(x), 2, "e4m3") @ unpack4(w1_words, w1_scales)) + f64(b1)) * f64(g)
    logits = mxq(a, 2, "e4m3") @ unpack4(e_words, e_scales)
    lp = logits - logsumexp(logits, 2, True)
    sc = f64(score)
    prior = sc - logsumexp(sc, 1, True)
    return logsumexp(prior[:, :, None] + lp, 1, False) + np.log(vocab)


def setup_inputs():
    drawn = draw0()
    full = np.asarray(drawn['x']).astype(np.float64)
    scale = (np.abs(full).reshape(256, 4, 8, 128).max(axis=(3,)) / 448.0).astype(np.float32)
    given = {}
    for key, value in drawn.items():
        if key == 'x':
            given['x_bytes'] = e4m3fn_bytes(full / np.repeat(scale.astype(np.float64), 128, axis=2))
            given['x_scale'] = scale
        else:
            given[key] = value
    return given


def reference(x_bytes, x_scale, w1_words, w1_scales, b1, g, e_words, e_scales, score):
    return core(e4m3fn_values(x_bytes) * np.repeat(x_scale.astype(np.float64), 128, axis=2), w1_words, w1_scales, b1, g, e_words, e_scales, score)

from contextlib import ExitStack

import concourse.mybir as mybir
from concourse.masks import make_identity

N, Z, D, H, V = 256, 4, 1024, 1024, 2048
FLOPS = 2 * N * Z * D * H + 2 * N * Z * H * V

F32 = mybir.dt.float32
BF16 = mybir.dt.bfloat16
I32 = mybir.dt.int32
U32 = mybir.dt.uint32
U8 = mybir.dt.uint8
FP8 = mybir.dt.float8_e4m3fn
FP8X4 = mybir.dt.float8_e4m3fn_x4
FP4X4 = mybir.dt.float4_e2m1fn_x4
ALU = mybir.AluOpType
ACT = mybir.ActivationFunctionType
AX = mybir.AxisListType

P = 128
HALVES = N // P
CH = V // 512
V_CHUNKS = {0: 3, 1: 2}


def tile_ragtokendocumentmarginal_d1p_kernel(
    tc, x_bytes, x_scale, w1_words, w1_scales, b1, g, e_words, e_scales, score, out
):
    nc = tc.nc
    with ExitStack() as ctx:
        keep = ctx.enter_context(tc.tile_pool(name="keep", bufs=1))
        work = ctx.enter_context(tc.tile_pool(name="work", bufs=4))
        psum = ctx.enter_context(tc.psum_pool(name="psum", bufs=8))

        xs = keep.tile([P, HALVES, 32], F32, name="xs")
        xb = [keep.tile([P, Z, D], U8, name=f"xb{h}") for h in range(HALVES)]
        w_raw = keep.tile([P, 2, 2 * H], U8, name="w_raw", align_bytes=64)
        ws_raw = keep.tile([P, 2, H], U8, name="ws_raw", align_bytes=64)
        ew = keep.tile([P, 2, 2 * V], U8, name="ew", align_bytes=64)
        es = keep.tile([P, 2, V], U8, name="es", align_bytes=64)
        b_sb = keep.tile([P, 2, 4], BF16, name="b_sb")
        g_sb = keep.tile([P, 2, 4], BF16, name="g_sb")
        sc = keep.tile([P, HALVES, Z], BF16, name="sc")
        ident = keep.tile([P, P], F32, name="ident")

        nc.vector.memset(ws_raw[:].rearrange("p g n -> p (g n)").bitcast(I32), 0)
        nc.gpsimd.memset(es[:].rearrange("p g n -> p (g n)").bitcast(I32), 0)
        make_identity(nc, ident[:])

        nc.scalar.dma_start(out=xs[:], in_=x_scale.rearrange("(h n) z j -> n h (z j)", h=HALVES))
        nc.sync.dma_start(out=xb[0][:, 0, :], in_=x_bytes[0:P, 0, :])
        nc.sync.dma_start(
            out=w_raw[:].rearrange("p g n -> p (g n)").bitcast(I32).rearrange("p (g n) -> p g n", g=2),
            in_=w1_words.bitcast(I32).rearrange("g p n -> p g n"),
        )
        nc.sync.dma_start(out=xb[0][:, 1:Z, :], in_=x_bytes[0:P, 1:Z, :])
        wsi = ws_raw[:].rearrange("p g n -> p (g n)").bitcast(I32).rearrange("p (g n) -> p g n", g=2)
        for q in range(4):
            nc.sync.dma_start(
                out=wsi[32 * q : 32 * q + 4],
                in_=w1_scales.bitcast(I32)[:, 4 * q : 4 * q + 4, :].rearrange("g r n -> r g n"),
            )
        nc.scalar.dma_start(out=b_sb[:], in_=b1.rearrange("(c p t) -> p c t", p=P, t=4))
        nc.scalar.dma_start(out=g_sb[:], in_=g.rearrange("(c p t) -> p c t", p=P, t=4))
        nc.scalar.dma_start(out=sc[:], in_=score.rearrange("(h n) z -> n h z", h=HALVES))
        nc.sync.dma_start(out=xb[1][:], in_=x_bytes[P : 2 * P, :, :])
        esi = es[:].rearrange("p g n -> p (g n)").bitcast(I32).rearrange("p (g n) -> p g n", g=2)
        for q in range(4):
            nc.sync.dma_start(
                out=esi[32 * q : 32 * q + 4],
                in_=e_scales.bitcast(I32)[:, 4 * q : 4 * q + 4, :].rearrange("g r n -> r g n"),
            )
        nc.sync.dma_start(
            out=ew[:].rearrange("p g n -> p (g n)").bitcast(I32).rearrange("p (g n) -> p g n", g=2),
            in_=e_words.bitcast(I32).rearrange("g p n -> p g n"),
        )

        wp = keep.tile([P, 2, 2, 4, P, 2], U8, name="wp", align_bytes=64)
        wsp = keep.tile([P, 2, 2, 4, P], U8, name="wsp", align_bytes=64)
        for c in range(2):
            for k in range(2):
                nc.vector.tensor_copy(
                    out=wp[:, c, k],
                    in_=w_raw[:, k, 1024 * c : 1024 * (c + 1)].rearrange("p (m t b) -> p t m b", t=4, b=2),
                )
                nc.vector.tensor_copy(
                    out=wsp[:, c, k],
                    in_=ws_raw[:, k, 512 * c : 512 * (c + 1)].rearrange("p (m t) -> p t m", t=4),
                )

        xq = [keep.tile([P, 2, Z * P], U32, name=f"xq{h}", align_bytes=64) for h in range(HALVES)]
        xqs = [keep.tile([P, 2, Z * P], U8, name=f"xqs{h}", align_bytes=64) for h in range(HALVES)]
        xg = [keep.tile([P, 2, Z, P, 2], F32, name=f"xg{h}", align_bytes=64) for h in range(HALVES)]

        def x_prepare(h, z, on_vector, evacuate_on_vector):
            xw = work.tile([P, D], BF16, tag="xw", name="xw")
            for j in range(8):
                src = xb[h][:, z, P * j : P * (j + 1)].bitcast(FP8)
                scale = xs[:, h, 8 * z + j : 8 * z + j + 1]
                if j not in on_vector:
                    nc.scalar.activation(xw[:, P * j : P * (j + 1)], src, ACT.Copy, scale=scale)
                else:
                    nc.vector.tensor_scalar(xw[:, P * j : P * (j + 1)], src, scale, None, ALU.mult)
            bank = psum.tile([P, 2, 2, P], F32, tag="ps", name="tr")
            words = xw[:].bitcast(F32)
            for k in range(2):
                for u in range(2):
                    nc.tensor.transpose(bank[:, k, u, :], words[:, 256 * k + u : 256 * (k + 1) : 2], ident[:])
            dst = xg[h][:, :, z]
            view = bank[:].rearrange("p k u r -> p k r u")
            if not evacuate_on_vector:
                nc.scalar.copy(dst, view)
            else:
                nc.vector.tensor_copy(out=dst, in_=view)

        def x_quantize(h, zp):
            for k in range(2):
                cols = slice(2 * P * zp, 2 * P * (zp + 1))
                nc.vector.quantize_mx(
                    out=xq[h][:, k, cols].bitcast(FP8X4),
                    scales=xqs[h][:, k, cols],
                    in_=xg[h][:, k, 2 * zp : 2 * zp + 2].rearrange("p z r u -> p (z r u)").bitcast(BF16),
                )

        aq = [keep.tile([P, 2, Z * P], U32, name=f"aq{h}", align_bytes=64) for h in range(HALVES)]
        aqs = [keep.tile([P, 2, Z * P], U8, name=f"aqs{h}", align_bytes=64) for h in range(HALVES)]
        th = {}

        def stage1(h, c):
            th[h, c] = work.tile([P, 4, Z * P], F32, tag="th", name="th")
            for t in range(4):
                bank = psum.tile([P, Z * P], F32, tag="ps", name="hid")
                for k in range(2):
                    nc.tensor.matmul_mx(
                        out=bank[:],
                        lhsT=wp[:, c, k, t].rearrange("p m b -> p (m b)").bitcast(FP4X4),
                        lhsT_scale=wsp[:, c, k, t],
                        rhs=xq[h][:, k, :].bitcast(FP8X4),
                        rhs_scale=xqs[h][:, k, :],
                        start=(k == 0),
                        stop=(k == 1),
                    )
                nc.scalar.activation(th[h, c][:, t, :], bank[:], ACT.Tanh, bias=b_sb[:, c, t : t + 1])

        ag = {}

        def gain(h, c, zp):
            ag[h, c, zp] = work.tile([P, 2 * P, 4], BF16, tag="ag", name="ag", align_bytes=64)
            cols = slice(2 * P * zp, 2 * P * (zp + 1))
            nc.vector.tensor_tensor(
                out=ag[h, c, zp][:],
                in0=th[h, c][:, :, cols].rearrange("p t n -> p n t"),
                in1=g_sb[:, c, :].unsqueeze(1).to_broadcast([P, 2 * P, 4]),
                op=ALU.mult,
            )

        def a_quantize(h, c, zp):
            cols = slice(2 * P * zp, 2 * P * (zp + 1))
            nc.vector.quantize_mx(
                out=aq[h][:, c, cols].bitcast(FP8X4),
                scales=aqs[h][:, c, cols],
                in_=ag[h, c, zp][:].rearrange("p n t -> p (n t)"),
            )

        prior = keep.tile([P, HALVES, Z], F32, name="prior")
        pmax = keep.tile([P, HALVES], F32, name="pmax")
        psub = keep.tile([P, HALVES, Z], F32, name="psub")
        pexp = keep.tile([P, HALVES, Z], F32, name="pexp")
        psum_z = keep.tile([P, HALVES], F32, name="psum_z")
        prec = keep.tile([P, HALVES], F32, name="prec")

        def make_prior():
            nc.vector.tensor_reduce(out=pmax[:], in_=sc[:], axis=AX.X, op=ALU.max)
            nc.vector.tensor_tensor(
                out=psub[:], in0=sc[:], in1=pmax[:].unsqueeze(2).to_broadcast([P, HALVES, Z]), op=ALU.subtract
            )
            nc.scalar.activation(pexp[:], psub[:], ACT.Exp)
            nc.vector.tensor_reduce(out=psum_z[:], in_=pexp[:], axis=AX.X, op=ALU.add)
            nc.vector.reciprocal(out=prec[:], in_=psum_z[:])
            nc.vector.tensor_tensor(
                out=prior[:], in0=pexp[:], in1=prec[:].unsqueeze(2).to_broadcast([P, HALVES, Z]), op=ALU.mult
            )

        rows = {}
        weight = {}
        diag = {}

        def stage2(z):
            nm = work.tile([P, HALVES, CH], F32, tag="nm", name="nm")
            s4 = work.tile([P, HALVES, CH], F32, tag="s4", name="s4")
            for h in range(HALVES):
                row = work.tile([P, V], F32, tag="row", name="row", bufs=8)
                rows[h, z] = row
                for c in range(CH):
                    bank = psum.tile([P, 512], F32, tag="ps", name="log")
                    for k in range(2):
                        nc.tensor.matmul_mx(
                            out=bank[:],
                            lhsT=aq[h][:, k, P * z : P * (z + 1)].bitcast(FP8X4),
                            lhsT_scale=aqs[h][:, k, P * z : P * (z + 1)],
                            rhs=ew[:, k, 1024 * c : 1024 * (c + 1)].bitcast(FP4X4),
                            rhs_scale=es[:, k, 512 * c : 512 * (c + 1)],
                            start=(k == 0),
                            stop=(k == 1),
                        )
                    nc.vector.tensor_reduce(out=nm[:, h, c : c + 1], in_=bank[:], axis=AX.X, op=ALU.max, negate=True)
                    nc.scalar.activation(
                        row[:, 512 * c : 512 * (c + 1)], bank[:], ACT.Exp,
                        bias=nm[:, h, c : c + 1], accum_out=s4[:, h, c : c + 1],
                    )
            nb = work.tile([P, HALVES], F32, tag="nb", name="nb")
            e4 = work.tile([P, HALVES, CH], F32, tag="e4", name="e4")
            ep = work.tile([P, HALVES, CH], F32, tag="ep", name="ep")
            se = work.tile([P, HALVES, CH], F32, tag="se", name="se")
            ss = work.tile([P, HALVES], F32, tag="ss", name="ss")
            rc = work.tile([P, HALVES], F32, tag="rc", name="rc")
            wt = work.tile([P, HALVES, CH], F32, tag="wt", name="wt")
            weight[z] = wt
            nc.vector.tensor_reduce(out=nb[:], in_=nm[:], axis=AX.X, op=ALU.min)
            for h in range(HALVES):
                nc.scalar.activation(e4[:, h, :], nm[:, h, :], ACT.Exp, bias=nb[:, h : h + 1], scale=-1.0)
            nc.vector.tensor_tensor(
                out=ep[:], in0=e4[:], in1=prior[:, :, z : z + 1].to_broadcast([P, HALVES, CH]), op=ALU.mult
            )
            nc.vector.tensor_tensor(out=se[:], in0=s4[:], in1=e4[:], op=ALU.mult)
            nc.vector.tensor_reduce(out=ss[:], in_=se[:], axis=AX.X, op=ALU.add)
            nc.vector.reciprocal(out=rc[:], in_=ss[:])
            nc.vector.tensor_tensor(
                out=wt[:], in0=ep[:], in1=rc[:].unsqueeze(2).to_broadcast([P, HALVES, CH]), op=ALU.mult
            )
            for h in range(HALVES):
                for c in range(V_CHUNKS[h], CH):
                    d = work.tile([P, P], F32, tag="diag", name="diag", bufs=8)
                    diag[h, z, c] = d
                    nc.gpsimd.tensor_scalar(d[:], ident[:], wt[:, h, c : c + 1], 0.0, ALU.mult, ALU.add)

        acc = {}

        def combine(z):
            for h in range(HALVES):
                for c in range(CH):
                    p = rows[h, z][:, 512 * c : 512 * (c + 1)]
                    w = weight[z][:, h, c : c + 1]
                    if c >= V_CHUNKS[h]:
                        if z == 0:
                            acc[h, c] = psum.tile([P, 512], F32, tag="ps", name="mix")
                        nc.tensor.matmul(acc[h, c][:], lhsT=diag[h, z, c][:], rhs=p, start=(z == 0), stop=(z == Z - 1))
                    elif z == 0:
                        acc[h, c] = keep.tile([P, 512], F32, name=f"acc{h}{c}")
                        nc.vector.tensor_scalar(acc[h, c][:], p, w, None, ALU.mult)
                    else:
                        nc.vector.scalar_tensor_tensor(
                            out=acc[h, c][:], in0=p, scalar=w, in1=acc[h, c][:], op0=ALU.mult, op1=ALU.add
                        )

        def finish(h, c):
            o = work.tile([P, 512], F32, tag="o", name="o")
            nc.scalar.activation(o[:], acc[h, c][:], ACT.Ln, scale=float(V))
            nc.sync.dma_start(out=out[P * h : P * (h + 1), 512 * c : 512 * (c + 1)], in_=o[:])

        on_v = (0, 2, 4, 6)
        for h in range(HALVES):
            for z in range(Z):
                x_prepare(h, z, on_v, h == 0 and z % 2 == 1)
                if z % 2 == 1:
                    x_quantize(h, z // 2)
        make_prior()
        for c in range(2):
            for h in range(HALVES):
                stage1(h, c)
                for zp in range(2):
                    gain(h, c, zp)
                    a_quantize(h, c, zp)
        stage2(0)
        for z in range(1, Z):
            stage2(z)
            combine(z - 1)
        combine(Z - 1)
        for c in reversed(range(CH)):
            for h in range(HALVES):
                finish(h, c)
